import numpy as np
import ml_dtypes


def mxq(x, axis, fmt="e4m3"):
    dtype, down = {"e4m3": (ml_dtypes.float8_e4m3fn, 7), "e5m2": (ml_dtypes.float8_e5m2, 14)}[fmt]
    v = np.moveaxis(np.asarray(x, np.float32).astype(ml_dtypes.bfloat16).astype(np.float64), axis, -1)
    blocks = v.reshape(v.shape[:-1] + (-1, 32))
    amax = np.abs(blocks).max(-1, keepdims=True)
    byte = np.maximum(np.where(amax > 0, np.frexp(amax)[1] - 1 + 127, 0) - down, 1)
    scale = np.exp2(byte - 127.0)
    codes = (blocks / scale).astype(np.float32).astype(dtype).astype(np.float64)
    return np.moveaxis((codes * scale).reshape(v.shape), -1, axis)


WIDE = False


def mx_kscale(k):
    if not WIDE:
        return np.ones(k)
    levels = np.array([10, -10, 5, -5, 0])
    if k % 512:
        return np.exp2(np.random.permutation(np.resize(levels, k // 32))).repeat(32)
    a = np.empty((k // 512, 16))
    for p in range(k // 512):
        a[p, :8] = np.random.permutation(np.resize(levels, 8))
        for g in range(8):
            far = levels[np.abs(levels - a[p, g]) >= 10]
            a[p, g + 8] = far[np.random.randint(len(far))]
    return np.exp2(a.ravel()).repeat(32)


def f64(x):
    return np.asarray(x).astype(np.float64)


def striped(idx):
    return np.tile(idx.reshape(-1, 16).T, (8, 1)).astype(np.uint16)


def unstriped(offs):
    return offs[:16].T.reshape(-1).astype(np.int64)


E2M1 = np.array([0.0, 0.5, 1.0, 1.5, 2.0, 3.0, 4.0, 6.0, -0.0, -0.5, -1.0, -1.5, -2.0, -3.0, -4.0, -6.0])


def pack_weight(w, fmt):
    k, n = w.shape
    w = f64(np.asarray(w, np.float32).astype(ml_dtypes.bfloat16)).reshape(k // 32, 32, n)
    amax = np.abs(w).max(1)
    if fmt == "e4m3":
        byte = np.frexp(amax)[1] - 1 + 127 - 7
    else:
        mant, ex = np.frexp(amax / 6.0)
        byte = np.where(mant > 0.5, ex, ex - 1) + 127
    byte = np.clip(np.where(amax > 0, byte, 1), 1, 254)
    scaled = (w * np.exp2(127.0 - byte)[:, None, :]).reshape(k, n).astype(np.float32)
    by_word = np.ascontiguousarray(scaled.reshape(k // 512, 128, 4, n).transpose(0, 1, 3, 2))
    if fmt == "e4m3":
        words = by_word.astype(ml_dtypes.float8_e4m3fn).view(np.uint8)
    else:
        c = by_word.astype(ml_dtypes.float4_e2m1fn).view(np.uint8) & 0xF
        words = (c[..., 0::2] | (c[..., 1::2] << 4)).reshape(k // 512, 128, 2 * n)
    return np.ascontiguousarray(words), np.ascontiguousarray(byte.astype(np.uint8).reshape(k // 512, 16, n))


def unpack_weight(words, scales, fmt):
    g, _, n = scales.shape
    words = np.ascontiguousarray(words).reshape(g, 128, n, -1)
    if fmt == "e4m3":
        vals = words.view(ml_dtypes.float8_e4m3fn).astype(np.float64)
    else:
        nib = np.empty((g, 128, n, 4), np.uint8)
        nib[..., 0::2] = words & 0xF
        nib[..., 1::2] = words >> 4
        vals = E2M1[nib]
    vals = vals * np.repeat(np.exp2(scales.astype(np.float64) - 127.0), 8, axis=1)[..., None]
    return vals.transpose(0, 1, 3, 2).reshape(g * 512, n)


def gelu(v):
    return 0.5 * v * (1.0 + np.tanh(np.sqrt(2.0 / np.pi) * (v + 0.044715 * v**3)))


def often(T, S):
    return np.random.permutation(T)[(T * np.random.uniform(0, 1, S) ** 4).astype(np.int64)]


K, K2, T, S, P, H, N = 1024, 512, 2048, 1024, 512, 1024, 512

def setup_inputs():
    n = np.random.standard_normal
    s = mx_kscale(K)[:, None]
    s2 = mx_kscale(K2)[:, None]
    u = mx_kscale(H)[:, None]
    d = {}
    d["tab_words"], d["tab_scales"] = pack_weight(n((K, T)) * s, "e4m3")
    d["tab2_words"], d["tab2_scales"] = pack_weight(n((K2, T)) * s2, "e4m3")
    d["tab3_words"], d["tab3_scales"] = pack_weight(n((K2, T)) * s2, "e4m3")
    d["offs"] = striped(np.random.permutation(T)[:S])
    d["offs2"] = striped(np.random.permutation(T)[:S])
    d["offs3"] = striped(np.random.permutation(T)[:S])
    d["pos1"] = striped(np.random.permutation(S)[:P])
    d["pos2"] = striped(often(S, P))
    d["pos3"] = striped(often(S, P))
    d["w1_words"], d["w1_scales"] = pack_weight(1.5 * n((K, H)) / K**0.5 / s * u.T, "e2m1")
    d["w2"] = (2.0 * n((K2, H)) / K2**0.5 / s2).astype(np.float32)
    d["b2"] = (0.7 * n(H)).astype(np.float32)
    d["w3"] = (0.8 * n((K2, H)) / K2**0.5 / s2 * u.T).astype(np.float32)
    d["w4"] = (1.3 * n((H, N)) / H**0.5 / u).astype(np.float32)
    d["w5_words"], d["w5_scales"] = pack_weight(1.6 * n((H, N)) / H**0.5 / u, "e4m3")
    d["b5"] = (0.5 * n(N)).astype(np.float32)
    return d

def reference(tab_words, tab_scales, tab2_words, tab2_scales, tab3_words, tab3_scales, offs, offs2, offs3, pos1, pos2, pos3, w1_words, w1_scales, w2, b2, w3, w4, w5_words, w5_scales, b5):
    v = unpack_weight(tab_words, tab_scales, "e4m3")[:, unstriped(offs)]
    v2 = unpack_weight(tab2_words, tab2_scales, "e4m3")[:, unstriped(offs2)]
    v3 = unpack_weight(tab3_words, tab3_scales, "e4m3")[:, unstriped(offs3)]
    a = unpack_weight(w1_words, w1_scales, "e2m1").T @ v
    b = (mxq(f64(w2), 0, "e4m3").T @ v2) + f64(b2)[:, None]
    d = mxq(f64(w3), 0, "e4m3").T @ v3
    x = d[:, unstriped(pos3)]
    fit = 1.0 / (1.0 + np.exp(-b[:, unstriped(pos2)]))
    z = a[:, unstriped(pos1)] * fit - x
    y = mxq(f64(w4), 0, "e4m3").T @ mxq(z, 0, "e4m3")
    e = unpack_weight(w5_words, w5_scales, "e4m3").T @ mxq(x, 0, "e4m3")
    return y * np.tanh(e + f64(b5)[:, None])

@@ -1,0 +1,270 @@
+from contextlib import ExitStack
+
+import concourse.mybir as mybir
+
+K, K2, T, S, R, H, N = 1024, 512, 2048, 1024, 512, 1024, 512
+FLOPS = 2 * (K * H * S + 2 * K2 * H * S + 2 * H * N * R)
+
+F32 = mybir.dt.float32
+BF16 = mybir.dt.bfloat16
+I32 = mybir.dt.int32
+U32 = mybir.dt.uint32
+U16 = mybir.dt.uint16
+U8 = mybir.dt.uint8
+FP8X4 = mybir.dt.float8_e4m3fn_x4
+FP4X4 = mybir.dt.float4_e2m1fn_x4
+ACT = mybir.ActivationFunctionType
+ALU = mybir.AluOpType
+
+P = 128
+PACK = 4
+PASS = P * PACK
+BANK = 512
+HALF = 256
+
+
+def tile_list_costume_hire_features_kernel(
+    tc, tab_words, tab_scales, tab2_words, tab2_scales, tab3_words, tab3_scales, offs, offs2, offs3,
+    pos1, pos2, pos3, w1_words, w1_scales, w2, b2, w3, w4, w5_words, w5_scales, b5, out,
+):
+    nc = tc.nc
+    with ExitStack() as ctx:
+        lists = ctx.enter_context(tc.tile_pool(name="lists", bufs=1))
+        keep = ctx.enter_context(tc.tile_pool(name="keep", bufs=1))
+        ring = ctx.enter_context(tc.tile_pool(name="ring", bufs=1))
+        psum = ctx.enter_context(tc.psum_pool(name="psum", bufs=8))
+
+        def load_list(src, name):
+            t = lists.tile(list(src.shape), U16, name=name)
+            nc.sync.dma_start(t[:], src)
+            return t
+
+        def zeroed_plane(width, name, engine):
+            t = keep.tile([P, width], U8, name=name, align_bytes=64)
+            engine.memset(t[:].bitcast(I32), 0)
+            return t
+
+        def load_table_scales(plane, scales):
+            passes = scales.shape[0]
+            for q in range(4):
+                src = scales[:, 4 * q : 4 * q + 4, :] if passes > 1 else scales[0, 4 * q : 4 * q + 4, :]
+                nc.sync.dma_start(plane[32 * q : 32 * q + 4 * passes, :].bitcast(I32), src.bitcast(I32))
+
+        def load_weight_scales(plane, scales):
+            for q in range(4):
+                nc.sync.dma_start(
+                    plane[32 * q : 32 * q + 4, :].rearrange("r (a c) -> r a c", a=2).bitcast(I32),
+                    scales[:, 4 * q : 4 * q + 4, :].rearrange("a r c -> r a c").bitcast(I32),
+                )
+
+        def load_words(words, name):
+            t = keep.tile([P, words.shape[1]], I32, name=name, align_bytes=64)
+            nc.sync.dma_start(t[:], words.rearrange("p t i -> p (t i)").bitcast(I32))
+            return t
+
+        def load_rows(rows, tag="raw", bufs=3):
+            raw = ring.tile([P, PACK, rows.shape[1]], F32, name=tag, bufs=bufs)
+            nc.sync.dma_start(raw[:], rows.rearrange("(p j) c -> p j c", j=PACK))
+            return raw
+
+        def gather_bytes(window, offsets, dtype, name):
+            t = keep.tile([P, S], dtype, name=name, align_bytes=64)
+            nc.vector.tensor_copy(t[:], window[:].bitcast(dtype).indirect(offsets[:]))
+            return t
+
+        def grouped_tile():
+            return ring.tile([P, PACK * BANK], BF16, name="grouped", bufs=3, align_bytes=64)
+
+        def quantize(grouped, name):
+            width = grouped.shape[1] // PACK
+            codes = keep.tile([P, width], U32, name=name + "_codes", align_bytes=64)
+            scales = keep.tile([P, width], U8, name=name + "_scales", align_bytes=64)
+            nc.vector.quantize_mx(out=codes[:].bitcast(FP8X4), scales=scales[:], in_=grouped[:])
+            return codes, scales
+
+        def quantize_dealt(parts, name):
+            g = grouped_tile()
+            dealt = g[:].rearrange("p (t m j) -> p m j t", t=PACK, j=PACK)
+            m0 = 0
+            for raw in parts:
+                m1 = m0 + raw.shape[2] // PACK
+                nc.scalar.copy(dealt[:, m0:m1], raw[:].rearrange("p j (m t) -> p m j t", t=PACK))
+                m0 = m1
+            return quantize(g, name)
+
+        def woven(g):
+            return g[:].rearrange("p (c i t) -> p c t i", i=4, t=PACK)
+
+        def planes(raw):
+            return raw[:].rearrange("p t (c i) -> p c t i", i=4)
+
+        def quantize_plain(raw, name):
+            g = grouped_tile()
+            nc.scalar.copy(woven(g), planes(raw))
+            return quantize(g, name)
+
+        def first_stage(operands, evacuate):
+            res = ring.tile([P, S], F32, name="first", bufs=9)
+            for h in range(S // BANK):
+                cols = slice(h * BANK, (h + 1) * BANK)
+                bank = psum.tile([P, BANK], F32, name="bank")
+                for n, (lhs, lhs_scale, rhs, rhs_scale) in enumerate(operands):
+                    nc.tensor.matmul_mx(
+                        out=bank[:], lhsT=lhs, lhsT_scale=lhs_scale, rhs=rhs[:, cols].bitcast(FP8X4),
+                        rhs_scale=rhs_scale[:, cols], start=(n == 0), stop=(n == len(operands) - 1),
+                    )
+                evacuate(res[:, cols], bank[:])
+            return res
+
+        s3_win = zeroed_plane(T, "s3_win", nc.gpsimd)
+        s2_win = zeroed_plane(T, "s2_win", nc.gpsimd)
+        s1_win = zeroed_plane(T, "s1_win", nc.gpsimd)
+        w1_sc_raw = zeroed_plane(H, "w1_sc_raw", nc.gpsimd)
+        w1_sc_pass1 = zeroed_plane(H, "w1_sc_pass1", nc.gpsimd)
+        v1_sc_pass1 = zeroed_plane(S, "v1_sc_pass1", nc.gpsimd)
+        w5_sc = zeroed_plane(2 * N, "w5_sc", nc.gpsimd)
+
+        offs3_t = load_list(offs3, "offs3")
+        offs2_t = load_list(offs2, "offs2")
+        w3_first = [load_rows(w3[:, 0:HALF], "raw_half", 2)]
+        load_table_scales(s3_win, tab3_scales)
+        t3_win = load_words(tab3_words[0], "t3_win")
+        w3_first.append(load_rows(w3[:, HALF:PASS], "raw_half", 2))
+        load_table_scales(s2_win, tab2_scales)
+        w3_second = load_rows(w3[:, PASS : 2 * PASS])
+        pos3_t = load_list(pos3, "pos3")
+        offs_t = load_list(offs, "offs")
+        load_table_scales(s1_win, tab_scales)
+        t2_win = load_words(tab2_words[0], "t2_win")
+        load_table_scales(w1_sc_raw, w1_scales)
+        w2_raw = [load_rows(w2[:, 0:PASS])]
+        t1_win = [load_words(tab_words[0], "t1_win0")]
+        w1_raw = keep.tile([P, 2, H // 2], I32, name="w1_raw", align_bytes=64)
+        nc.sync.dma_start(w1_raw[:], w1_words.rearrange("a p c -> p a c").bitcast(I32))
+        t1_win.append(load_words(tab_words[1], "t1_win1"))
+
+        v3_sc = gather_bytes(s3_win, offs3_t, U8, "v3_sc")
+        v3 = gather_bytes(t3_win, offs3_t, U32, "v3")
+        w3_q = [quantize_dealt(w3_first, "w3q0"), quantize_dealt([w3_second], "w3q1")]
+        v2_sc = gather_bytes(s2_win, offs2_t, U8, "v2_sc")
+        v1_sc = gather_bytes(s1_win, offs_t, U8, "v1_sc")
+        nc.sync.dma_start(v1_sc_pass1[0:112, :].bitcast(I32), v1_sc[4:116, :].bitcast(I32))
+        w1_sc = keep.tile([P, H], U8, name="w1_sc", align_bytes=64)
+        nc.vector.tensor_copy(
+            w1_sc[:].rearrange("p (b t m) -> p b t m", b=2, t=PACK),
+            w1_sc_raw[:].rearrange("p (b m t) -> p b t m", b=2, t=PACK),
+        )
+        nc.sync.dma_start(w1_sc_pass1[0:112, :].bitcast(I32), w1_sc[4:116, :].bitcast(I32))
+        w1_scale = [w1_sc, w1_sc_pass1]
+        v1_scales = [v1_sc, v1_sc_pass1]
+
+        pos2_t = load_list(pos2, "pos2")
+        pos1_t = load_list(pos1, "pos1")
+        b2_t = keep.tile([P, 2, PACK], F32, name="b2_t")
+        nc.sync.dma_start(b2_t[:], b2.rearrange("(b p t) -> p b t", b=2, t=PACK))
+        w2_raw.append(load_rows(w2[:, PASS : 2 * PASS]))
+        load_weight_scales(w5_sc, w5_scales)
+        w5_w = keep.tile([P, 2, N], I32, name="w5_w", align_bytes=64)
+        nc.sync.dma_start(w5_w[:], w5_words.rearrange("a p c i -> p a (c i)").bitcast(I32))
+        b5_t = keep.tile([P, N // P], F32, name="b5_t")
+        with nc.allow_non_contiguous_dma(reason="one bias value a partition and output tile"):
+            nc.sync.dma_start(b5_t[:], b5.rearrange("(u p) -> p u", p=P))
+        w4_raw = [load_rows(w4[a * PASS : (a + 1) * PASS, :]) for a in range(2)]
+
+        v2 = gather_bytes(t2_win, offs2_t, U32, "v2")
+        w1_p = keep.tile([P, 2, 2 * H], U8, name="w1_p", align_bytes=64)
+        nc.vector.tensor_copy(
+            w1_p[:].bitcast(U16).rearrange("p a (b t m) -> p (a b) t m", b=2, t=PACK),
+            w1_raw[:].bitcast(U16).rearrange("p a (b m t) -> p (a b) t m", b=2, t=PACK),
+        )
+        v1 = [gather_bytes(t1_win[a], offs_t, U32, "v1_%d" % a) for a in range(2)]
+
+        x = []
+        for b in range(2):
+            codes, scales = w3_q[b]
+            xb = keep.tile([P, PACK, R], F32, name="x%d" % b)
+            for t in range(PACK):
+                m = slice(t * P, (t + 1) * P)
+                d = first_stage([(codes[:, m].bitcast(FP8X4), scales[:, m], v3, v3_sc)], nc.scalar.copy)
+                nc.vector.tensor_copy(xb[:, t, :], d[:].indirect(pos3_t[:]))
+            x.append(xb)
+            if b == 0:
+                w2_q = [quantize_dealt([w2_raw[0]], "w2q0")]
+
+        x_q = [quantize_plain(x[0], "xq0")]
+        w2_q.append(quantize_dealt([w2_raw[1]], "w2q1"))
+        gate = keep.tile([P, N // P, R], F32, name="gate")
+
+        def gate_rows(u):
+            bank = psum.tile([P, BANK], F32, name="bank")
+            for a in range(2):
+                nc.tensor.matmul_mx(
+                    out=bank[:], lhsT=w5_w[:, a, u * P : (u + 1) * P].bitcast(FP8X4),
+                    lhsT_scale=w5_sc[:, a * N + u * P : a * N + (u + 1) * P],
+                    rhs=x_q[a][0][:].bitcast(FP8X4), rhs_scale=x_q[a][1][:], start=(a == 0), stop=(a == 1),
+                )
+            nc.scalar.activation(gate[:, u, :], bank[:], ACT.Tanh, bias=b5_t[:, u : u + 1])
+
+        def pick_fit(i):
+            b, t = divmod(i, PACK)
+            codes, scales = w2_q[b]
+            m = slice(t * P, (t + 1) * P)
+            fit = first_stage(
+                [(codes[:, m].bitcast(FP8X4), scales[:, m], v2, v2_sc)],
+                lambda dst, src: nc.scalar.activation(dst, src, ACT.Sigmoid, bias=b2_t[:, b, t : t + 1]),
+            )
+            picked = ring.tile([P, R], F32, name="picked_fit", bufs=3)
+            nc.vector.tensor_copy(picked[:], fit[:].indirect(pos2_t[:]))
+            return picked
+
+        z_q = []
+        w4_q = []
+        az = [keep.tile([P, PACK, R], F32, name="az%d" % b, tag=("t3_win", "t2_win")[b], align_bytes=64) for b in range(2)]
+        picked_next = pick_fit(0)
+        for i in range(2 * PACK):
+            b, t = divmod(i, PACK)
+            picked_fit = picked_next
+            if i + 1 < 2 * PACK:
+                picked_next = pick_fit(i + 1)
+            c0 = i * P
+            a_rows = first_stage(
+                [
+                    (w1_p[:, a, 2 * c0 : 2 * (c0 + P)].bitcast(FP4X4), w1_scale[a][:, c0 : c0 + P], v1[a], v1_scales[a])
+                    for a in range(2)
+                ],
+                nc.scalar.copy,
+            )
+            nc.vector.tensor_tensor(az[b][:, t, :], a_rows[:].indirect(pos1_t[:]), picked_fit[:], ALU.mult)
+            if i == 1:
+                x_q.append(quantize_plain(x[1], "xq1"))
+            if i in (3, 5):
+                w4_q.append(quantize_plain(w4_raw[len(w4_q)], "w4q%d" % len(w4_q)))
+            if t == PACK - 1:
+                halves = []
+                for h in range(2):
+                    cols = slice(h * HALF, (h + 1) * HALF)
+                    g = ring.tile([P, PACK * HALF], BF16, name="z_grouped", bufs=2, align_bytes=64)
+                    nc.vector.tensor_tensor(woven(g), planes(az[b][:, :, cols]), planes(x[b][:, :, cols]), ALU.subtract)
+                    halves.append(quantize(g, "zq%d%d" % (b, h)))
+                z_q.append(halves)
+        for u in range(N // P):
+            gate_rows(u)
+
+        for h in range(2):
+            cols = slice(h * HALF, (h + 1) * HALF)
+            for pair in range(2):
+                bank = psum.tile([P, BANK], F32, name="bank")
+                for i in range(2):
+                    m = slice((2 * pair + i) * P, (2 * pair + i + 1) * P)
+                    for a in range(2):
+                        nc.tensor.matmul_mx(
+                            out=bank[:, i * HALF : (i + 1) * HALF], lhsT=w4_q[a][0][:, m].bitcast(FP8X4),
+                            lhsT_scale=w4_q[a][1][:, m], rhs=z_q[a][h][0][:].bitcast(FP8X4),
+                            rhs_scale=z_q[a][h][1][:], start=(a == 0), stop=(a == 1),
+                        )
+                res = ring.tile([P, 2, HALF], F32, name="res", bufs=4)
+                nc.vector.tensor_tensor(
+                    res[:], bank[:].rearrange("p (i j) -> p i j", i=2), gate[:, 2 * pair : 2 * pair + 2, cols], ALU.mult
+                )
+                rows = out[2 * pair * P : 2 * (pair + 1) * P, cols]
+                nc.sync.dma_start(rows.rearrange("(i p) j -> p i j", p=P), res[:])

@@ -44,15 +44,15 @@ def tile_list_costume_hire_features_kernel(
             engine.memset(t[:].bitcast(I32), 0)
             return t
 
-        def load_table_scales(plane, scales):
+        def load_table_scales(plane, scales, queue):
             passes = scales.shape[0]
             for q in range(4):
                 src = scales[:, 4 * q : 4 * q + 4, :] if passes > 1 else scales[0, 4 * q : 4 * q + 4, :]
-                nc.sync.dma_start(plane[32 * q : 32 * q + 4 * passes, :].bitcast(I32), src.bitcast(I32))
+                queue.dma_start(plane[32 * q : 32 * q + 4 * passes, :].bitcast(I32), src.bitcast(I32))
 
         def load_weight_scales(plane, scales):
             for q in range(4):
-                nc.sync.dma_start(
+                nc.gpsimd.dma_start(
                     plane[32 * q : 32 * q + 4, :].rearrange("r (a c) -> r a c", a=2).bitcast(I32),
                     scales[:, 4 * q : 4 * q + 4, :].rearrange("a r c -> r a c").bitcast(I32),
                 )
@@ -88,15 +88,17 @@ def tile_list_costume_hire_features_kernel(
             m0 = 0
             for raw in parts:
                 m1 = m0 + raw.shape[2] // PACK
-                nc.scalar.copy(dealt[:, m0:m1], raw[:].rearrange("p j (m t) -> p m j t", t=PACK))
+                rows = raw[:].rearrange("p j (m t) -> p m j t", t=PACK)
+                for t0 in (0, 2):
+                    nc.scalar.copy(dealt[:, m0:m1, :, t0 : t0 + 2], rows[:, :, :, t0 : t0 + 2])
                 m0 = m1
             return quantize(g, name)
 
         def woven(g):
-            return g[:].rearrange("p (c i t) -> p c t i", i=4, t=PACK)
+            return g[:].rearrange("p (c i t) -> p c t i", i=2, t=PACK)
 
         def planes(raw):
-            return raw[:].rearrange("p t (c i) -> p c t i", i=4)
+            return raw[:].rearrange("p t (c i) -> p c t i", i=2)
 
         def quantize_plain(raw, name):
             g = grouped_tile()
@@ -119,25 +121,34 @@ def tile_list_costume_hire_features_kernel(
         s3_win = zeroed_plane(T, "s3_win", nc.gpsimd)
         s2_win = zeroed_plane(T, "s2_win", nc.gpsimd)
         s1_win = zeroed_plane(T, "s1_win", nc.gpsimd)
+        warm = keep.tile([P, 2], F32, name="warm")
+        nc.vector.memset(warm[:, 0:1], 0.0)
+        nc.scalar.activation(warm[:, 1:2], warm[:, 0:1], ACT.Sigmoid)
         w1_sc_raw = zeroed_plane(H, "w1_sc_raw", nc.gpsimd)
         w1_sc_pass1 = zeroed_plane(H, "w1_sc_pass1", nc.gpsimd)
         v1_sc_pass1 = zeroed_plane(S, "v1_sc_pass1", nc.gpsimd)
         w5_sc = zeroed_plane(2 * N, "w5_sc", nc.gpsimd)
+        load_weight_scales(w5_sc, w5_scales)
+        b2_t = keep.tile([P, 2, PACK], F32, name="b2_t")
+        nc.gpsimd.dma_start(b2_t[:], b2.rearrange("(b p t) -> p b t", b=2, t=PACK))
+        b5_t = keep.tile([P, N // P], F32, name="b5_t")
+        with nc.allow_non_contiguous_dma(reason="one bias value a partition and output tile"):
+            nc.gpsimd.dma_start(b5_t[:], b5.rearrange("(u p) -> p u", p=P))
 
         offs3_t = load_list(offs3, "offs3")
         offs2_t = load_list(offs2, "offs2")
         w3_first = [load_rows(w3[:, 0:HALF], "raw_half", 2)]
-        load_table_scales(s3_win, tab3_scales)
+        load_table_scales(s3_win, tab3_scales, nc.sync)
         t3_win = load_words(tab3_words[0], "t3_win")
         w3_first.append(load_rows(w3[:, HALF:PASS], "raw_half", 2))
-        load_table_scales(s2_win, tab2_scales)
+        load_table_scales(s2_win, tab2_scales, nc.sync)
         w3_second = load_rows(w3[:, PASS : 2 * PASS])
         pos3_t = load_list(pos3, "pos3")
         offs_t = load_list(offs, "offs")
-        load_table_scales(s1_win, tab_scales)
+        load_table_scales(s1_win, tab_scales, nc.sync)
         t2_win = load_words(tab2_words[0], "t2_win")
-        load_table_scales(w1_sc_raw, w1_scales)
-        w2_raw = [load_rows(w2[:, 0:PASS])]
+        w2_raw = [load_rows(w2[:, b * PASS : (b + 1) * PASS]) for b in range(2)]
+        load_table_scales(w1_sc_raw, w1_scales, nc.sync)
         t1_win = [load_words(tab_words[0], "t1_win0")]
         w1_raw = keep.tile([P, 2, H // 2], I32, name="w1_raw", align_bytes=64)
         nc.sync.dma_start(w1_raw[:], w1_words.rearrange("a p c -> p a c").bitcast(I32))
@@ -148,27 +159,20 @@ def tile_list_costume_hire_features_kernel(
         w3_q = [quantize_dealt(w3_first, "w3q0"), quantize_dealt([w3_second], "w3q1")]
         v2_sc = gather_bytes(s2_win, offs2_t, U8, "v2_sc")
         v1_sc = gather_bytes(s1_win, offs_t, U8, "v1_sc")
-        nc.sync.dma_start(v1_sc_pass1[0:112, :].bitcast(I32), v1_sc[4:116, :].bitcast(I32))
+        nc.gpsimd.dma_start(v1_sc_pass1[0:112, :].bitcast(I32), v1_sc[4:116, :].bitcast(I32))
         w1_sc = keep.tile([P, H], U8, name="w1_sc", align_bytes=64)
         nc.vector.tensor_copy(
             w1_sc[:].rearrange("p (b t m) -> p b t m", b=2, t=PACK),
             w1_sc_raw[:].rearrange("p (b m t) -> p b t m", b=2, t=PACK),
         )
-        nc.sync.dma_start(w1_sc_pass1[0:112, :].bitcast(I32), w1_sc[4:116, :].bitcast(I32))
+        nc.gpsimd.dma_start(w1_sc_pass1[0:112, :].bitcast(I32), w1_sc[4:116, :].bitcast(I32))
         w1_scale = [w1_sc, w1_sc_pass1]
         v1_scales = [v1_sc, v1_sc_pass1]
 
         pos2_t = load_list(pos2, "pos2")
         pos1_t = load_list(pos1, "pos1")
-        b2_t = keep.tile([P, 2, PACK], F32, name="b2_t")
-        nc.sync.dma_start(b2_t[:], b2.rearrange("(b p t) -> p b t", b=2, t=PACK))
-        w2_raw.append(load_rows(w2[:, PASS : 2 * PASS]))
-        load_weight_scales(w5_sc, w5_scales)
         w5_w = keep.tile([P, 2, N], I32, name="w5_w", align_bytes=64)
         nc.sync.dma_start(w5_w[:], w5_words.rearrange("a p c i -> p a (c i)").bitcast(I32))
-        b5_t = keep.tile([P, N // P], F32, name="b5_t")
-        with nc.allow_non_contiguous_dma(reason="one bias value a partition and output tile"):
-            nc.sync.dma_start(b5_t[:], b5.rearrange("(u p) -> p u", p=P))
         w4_raw = [load_rows(w4[a * PASS : (a + 1) * PASS, :]) for a in range(2)]
 
         v2 = gather_bytes(t2_win, offs2_t, U32, "v2")
@@ -235,9 +239,9 @@ def tile_list_costume_hire_features_kernel(
                 nc.scalar.copy,
             )
             nc.vector.tensor_tensor(az[b][:, t, :], a_rows[:].indirect(pos1_t[:]), picked_fit[:], ALU.mult)
-            if i == 1:
+            if i == 3:
                 x_q.append(quantize_plain(x[1], "xq1"))
-            if i in (3, 5):
+            if i in (5, 7):
                 w4_q.append(quantize_plain(w4_raw[len(w4_q)], "w4q%d" % len(w4_q)))
             if t == PACK - 1:
                 halves = []
@@ -247,24 +251,29 @@ def tile_list_costume_hire_features_kernel(
                     nc.vector.tensor_tensor(woven(g), planes(az[b][:, :, cols]), planes(x[b][:, :, cols]), ALU.subtract)
                     halves.append(quantize(g, "zq%d%d" % (b, h)))
                 z_q.append(halves)
+
         for u in range(N // P):
             gate_rows(u)
 
+        def y_pass(bank, u, h, a):
+            m = slice(u * P, (u + 1) * P)
+            nc.tensor.matmul_mx(
+                out=bank[:], lhsT=w4_q[a][0][:, m].bitcast(FP8X4), lhsT_scale=w4_q[a][1][:, m],
+                rhs=z_q[a][h][0][:].bitcast(FP8X4), rhs_scale=z_q[a][h][1][:], start=(a == 0), stop=(a == 1),
+            )
+
+        y = {}
+        for h in range(2):
+            for u in range(N // P):
+                y[h, u] = psum.tile([P, HALF], F32, name="bank")
+                y_pass(y[h, u], u, h, 0)
         for h in range(2):
             cols = slice(h * HALF, (h + 1) * HALF)
             for pair in range(2):
-                bank = psum.tile([P, BANK], F32, name="bank")
-                for i in range(2):
-                    m = slice((2 * pair + i) * P, (2 * pair + i + 1) * P)
-                    for a in range(2):
-                        nc.tensor.matmul_mx(
-                            out=bank[:, i * HALF : (i + 1) * HALF], lhsT=w4_q[a][0][:, m].bitcast(FP8X4),
-                            lhsT_scale=w4_q[a][1][:, m], rhs=z_q[a][h][0][:].bitcast(FP8X4),
-                            rhs_scale=z_q[a][h][1][:], start=(a == 0), stop=(a == 1),
-                        )
                 res = ring.tile([P, 2, HALF], F32, name="res", bufs=4)
-                nc.vector.tensor_tensor(
-                    res[:], bank[:].rearrange("p (i j) -> p i j", i=2), gate[:, 2 * pair : 2 * pair + 2, cols], ALU.mult
-                )
+                for i in range(2):
+                    u = 2 * pair + i
+                    y_pass(y[h, u], u, h, 1)
+                    nc.vector.tensor_tensor(res[:, i, :], y[h, u][:], gate[:, u, cols], ALU.mult)
                 rows = out[2 * pair * P : 2 * (pair + 1) * P, cols]
                 nc.sync.dma_start(rows.rearrange("(i p) j -> p i j", p=P), res[:])

@@ -44,22 +44,25 @@ def tile_list_costume_hire_features_kernel(
             engine.memset(t[:].bitcast(I32), 0)
             return t
 
-        def load_table_scales(plane, scales, queue):
+        def load_table_scales(plane, scales):
             passes = scales.shape[0]
             for q in range(4):
                 src = scales[:, 4 * q : 4 * q + 4, :] if passes > 1 else scales[0, 4 * q : 4 * q + 4, :]
-                queue.dma_start(plane[32 * q : 32 * q + 4 * passes, :].bitcast(I32), src.bitcast(I32))
+                nc.sync.dma_start(plane[32 * q : 32 * q + 4 * passes, :].bitcast(I32), src.bitcast(I32))
 
         def load_weight_scales(plane, scales):
             for q in range(4):
-                nc.gpsimd.dma_start(
+                nc.sync.dma_start(
                     plane[32 * q : 32 * q + 4, :].rearrange("r (a c) -> r a c", a=2).bitcast(I32),
                     scales[:, 4 * q : 4 * q + 4, :].rearrange("a r c -> r a c").bitcast(I32),
                 )
 
-        def load_words(words, name):
-            t = keep.tile([P, words.shape[1]], I32, name=name, align_bytes=64)
-            nc.sync.dma_start(t[:], words.rearrange("p t i -> p (t i)").bitcast(I32))
+        def merged(words):
+            return words.rearrange("p t i -> p (t i)")
+
+        def load_words(rows, name):
+            t = keep.tile([P, rows.shape[1] // 4], I32, name=name, align_bytes=64)
+            nc.sync.dma_start(t[:], rows.bitcast(I32))
             return t
 
         def load_rows(rows, tag="raw", bufs=3):
@@ -67,23 +70,22 @@ def tile_list_costume_hire_features_kernel(
             nc.sync.dma_start(raw[:], rows.rearrange("(p j) c -> p j c", j=PACK))
             return raw
 
-        def gather_bytes(window, offsets, dtype, name):
-            t = keep.tile([P, S], dtype, name=name, align_bytes=64)
+        def gather_bytes(window, offsets, dtype, name, tag=None):
+            t = keep.tile([P, S], dtype, name=name, tag=tag or name, align_bytes=64)
             nc.vector.tensor_copy(t[:], window[:].bitcast(dtype).indirect(offsets[:]))
             return t
 
         def grouped_tile():
             return ring.tile([P, PACK * BANK], BF16, name="grouped", bufs=3, align_bytes=64)
 
-        def quantize(grouped, name):
-            width = grouped.shape[1] // PACK
+        def quantize(g, name):
+            width = g.shape[1] // PACK
             codes = keep.tile([P, width], U32, name=name + "_codes", align_bytes=64)
             scales = keep.tile([P, width], U8, name=name + "_scales", align_bytes=64)
-            nc.vector.quantize_mx(out=codes[:].bitcast(FP8X4), scales=scales[:], in_=grouped[:])
+            nc.vector.quantize_mx(out=codes[:].bitcast(FP8X4), scales=scales[:], in_=g[:])
             return codes, scales
 
-        def quantize_dealt(parts, name):
-            g = grouped_tile()
+        def quantize_dealt(parts, name, g):
             dealt = g[:].rearrange("p (t m j) -> p m j t", t=PACK, j=PACK)
             m0 = 0
             for raw in parts:
@@ -100,13 +102,12 @@ def tile_list_costume_hire_features_kernel(
         def planes(raw):
             return raw[:].rearrange("p t (c i) -> p c t i", i=2)
 
-        def quantize_plain(raw, name):
-            g = grouped_tile()
+        def quantize_plain(raw, name, g):
             nc.scalar.copy(woven(g), planes(raw))
             return quantize(g, name)
 
         def first_stage(operands, evacuate):
-            res = ring.tile([P, S], F32, name="first", bufs=9)
+            res = ring.tile([P, S], F32, name="first", bufs=12)
             for h in range(S // BANK):
                 cols = slice(h * BANK, (h + 1) * BANK)
                 bank = psum.tile([P, BANK], F32, name="bank")
@@ -119,85 +120,106 @@ def tile_list_costume_hire_features_kernel(
             return res
 
         s3_win = zeroed_plane(T, "s3_win", nc.gpsimd)
-        s2_win = zeroed_plane(T, "s2_win", nc.gpsimd)
-        s1_win = zeroed_plane(T, "s1_win", nc.gpsimd)
+        s2_win = zeroed_plane(T, "s2_win", nc.vector)
+        s1_win = zeroed_plane(T, "s1_win", nc.vector)
         warm = keep.tile([P, 2], F32, name="warm")
         nc.vector.memset(warm[:, 0:1], 0.0)
         nc.scalar.activation(warm[:, 1:2], warm[:, 0:1], ACT.Sigmoid)
-        w1_sc_raw = zeroed_plane(H, "w1_sc_raw", nc.gpsimd)
-        w1_sc_pass1 = zeroed_plane(H, "w1_sc_pass1", nc.gpsimd)
-        v1_sc_pass1 = zeroed_plane(S, "v1_sc_pass1", nc.gpsimd)
-        w5_sc = zeroed_plane(2 * N, "w5_sc", nc.gpsimd)
-        load_weight_scales(w5_sc, w5_scales)
-        b2_t = keep.tile([P, 2, PACK], F32, name="b2_t")
-        nc.gpsimd.dma_start(b2_t[:], b2.rearrange("(b p t) -> p b t", b=2, t=PACK))
-        b5_t = keep.tile([P, N // P], F32, name="b5_t")
-        with nc.allow_non_contiguous_dma(reason="one bias value a partition and output tile"):
-            nc.gpsimd.dma_start(b5_t[:], b5.rearrange("(u p) -> p u", p=P))
+        w1_sc_raw = zeroed_plane(H, "w1_sc_raw", nc.vector)
+        w1_sc_pass1 = zeroed_plane(H, "w1_sc_pass1", nc.vector)
+        v1_sc_pass1 = zeroed_plane(S, "v1_sc_pass1", nc.vector)
+        w5_sc = zeroed_plane(2 * N, "w5_sc", nc.vector)
 
         offs3_t = load_list(offs3, "offs3")
         offs2_t = load_list(offs2, "offs2")
         w3_first = [load_rows(w3[:, 0:HALF], "raw_half", 2)]
-        load_table_scales(s3_win, tab3_scales, nc.sync)
-        t3_win = load_words(tab3_words[0], "t3_win")
+        load_table_scales(s3_win, tab3_scales)
+        t3_win = load_words(merged(tab3_words[0]), "t3_win")
         w3_first.append(load_rows(w3[:, HALF:PASS], "raw_half", 2))
-        load_table_scales(s2_win, tab2_scales, nc.sync)
-        w3_second = load_rows(w3[:, PASS : 2 * PASS])
-        pos3_t = load_list(pos3, "pos3")
+        load_table_scales(s2_win, tab2_scales)
+        t2_win = load_words(merged(tab2_words[0]), "t2_win")
         offs_t = load_list(offs, "offs")
-        load_table_scales(s1_win, tab_scales, nc.sync)
-        t2_win = load_words(tab2_words[0], "t2_win")
-        w2_raw = [load_rows(w2[:, b * PASS : (b + 1) * PASS]) for b in range(2)]
-        load_table_scales(w1_sc_raw, w1_scales, nc.sync)
-        t1_win = [load_words(tab_words[0], "t1_win0")]
+        load_table_scales(s1_win, tab_scales)
+        t1_win = [load_words(merged(tab_words[0]), "t1_win0")]
+        w3_second = load_rows(w3[:, PASS : 2 * PASS])
+        w2_raw = [load_rows(w2[:, 0:PASS])]
+        b2_t = keep.tile([P, 2, PACK], F32, name="b2_t")
+        nc.sync.dma_start(b2_t[:], b2.rearrange("(b p t) -> p b t", b=2, t=PACK))
         w1_raw = keep.tile([P, 2, H // 2], I32, name="w1_raw", align_bytes=64)
         nc.sync.dma_start(w1_raw[:], w1_words.rearrange("a p c -> p a c").bitcast(I32))
-        t1_win.append(load_words(tab_words[1], "t1_win1"))
+        load_table_scales(w1_sc_raw, w1_scales)
+        t1_win.append(load_words(merged(tab_words[1]), "t1_win1"))
+        pos3_t = load_list(pos3, "pos3")
+        pos1_t = load_list(pos1, "pos1")
 
         v3_sc = gather_bytes(s3_win, offs3_t, U8, "v3_sc")
         v3 = gather_bytes(t3_win, offs3_t, U32, "v3")
-        w3_q = [quantize_dealt(w3_first, "w3q0"), quantize_dealt([w3_second], "w3q1")]
+        w3_q = [quantize_dealt(w3_first, "w3q0", grouped_tile())]
         v2_sc = gather_bytes(s2_win, offs2_t, U8, "v2_sc")
-        v1_sc = gather_bytes(s1_win, offs_t, U8, "v1_sc")
-        nc.gpsimd.dma_start(v1_sc_pass1[0:112, :].bitcast(I32), v1_sc[4:116, :].bitcast(I32))
-        w1_sc = keep.tile([P, H], U8, name="w1_sc", align_bytes=64)
-        nc.vector.tensor_copy(
-            w1_sc[:].rearrange("p (b t m) -> p b t m", b=2, t=PACK),
-            w1_sc_raw[:].rearrange("p (b m t) -> p b t m", b=2, t=PACK),
-        )
-        nc.gpsimd.dma_start(w1_sc_pass1[0:112, :].bitcast(I32), w1_sc[4:116, :].bitcast(I32))
-        w1_scale = [w1_sc, w1_sc_pass1]
-        v1_scales = [v1_sc, v1_sc_pass1]
-
-        pos2_t = load_list(pos2, "pos2")
-        pos1_t = load_list(pos1, "pos1")
-        w5_w = keep.tile([P, 2, N], I32, name="w5_w", align_bytes=64)
-        nc.sync.dma_start(w5_w[:], w5_words.rearrange("a p c i -> p a (c i)").bitcast(I32))
-        w4_raw = [load_rows(w4[a * PASS : (a + 1) * PASS, :]) for a in range(2)]
-
         v2 = gather_bytes(t2_win, offs2_t, U32, "v2")
+        v1_sc = gather_bytes(s1_win, offs_t, U8, "v1_sc")
+        v1 = [gather_bytes(t1_win[0], offs_t, U32, "v1_0")]
+        w3_q.append(quantize_dealt([w3_second], "w3q1", grouped_tile()))
         w1_p = keep.tile([P, 2, 2 * H], U8, name="w1_p", align_bytes=64)
         nc.vector.tensor_copy(
-            w1_p[:].bitcast(U16).rearrange("p a (b t m) -> p (a b) t m", b=2, t=PACK),
-            w1_raw[:].bitcast(U16).rearrange("p a (b m t) -> p (a b) t m", b=2, t=PACK),
+            w1_p[:].bitcast(U16).rearrange("p a (b t g m) -> p (a b) g t m", b=2, t=PACK, m=8),
+            w1_raw[:].bitcast(U16).rearrange("p a (b g m t) -> p (a b) g t m", b=2, t=PACK, m=8),
         )
-        v1 = [gather_bytes(t1_win[a], offs_t, U32, "v1_%d" % a) for a in range(2)]
+        w2_q = [quantize_dealt([w2_raw[0]], "w2q0", grouped_tile())]
+        w1_sc = keep.tile([P, H], U8, name="w1_sc", align_bytes=64)
+        nc.vector.tensor_copy(
+            w1_sc[:].rearrange("p (b t g m) -> p b g t m", b=2, t=PACK, m=16),
+            w1_sc_raw[:].rearrange("p (b g m t) -> p b g t m", b=2, t=PACK, m=16),
+        )
+        v1.append(gather_bytes(t1_win[1], offs_t, U32, "v1_1"))
+        w1_scale = [w1_sc, w1_sc_pass1]
+        v1_scales = [v1_sc, v1_sc_pass1]
+        nc.sync.dma_start(v1_sc_pass1[0:112, :].bitcast(I32), v1_sc[4:116, :].bitcast(I32))
+        w2_raw.append(load_rows(w2[:, PASS : 2 * PASS]))
+        nc.sync.dma_start(w1_sc_pass1[0:112, :].bitcast(I32), w1_sc[4:116, :].bitcast(I32))
+        w4_raw = [load_rows(w4[0:PASS, :])]
+        pos2_t = load_list(pos2, "pos2")
+        w5_w = keep.tile([P, 2, N], I32, name="w5_w", align_bytes=64)
+        nc.sync.dma_start(w5_w[:], w5_words.rearrange("a p c i -> p a (c i)").bitcast(I32))
+        load_weight_scales(w5_sc, w5_scales)
+        w4_raw.append(load_rows(w4[PASS : 2 * PASS, :]))
+        b5_t = keep.tile([P, N // P], F32, name="b5_t")
+        with nc.allow_non_contiguous_dma(reason="one bias value a partition and output tile"):
+            nc.sync.dma_start(b5_t[:], b5.rearrange("(u p) -> p u", p=P))
 
-        x = []
-        for b in range(2):
-            codes, scales = w3_q[b]
-            xb = keep.tile([P, PACK, R], F32, name="x%d" % b)
-            for t in range(PACK):
-                m = slice(t * P, (t + 1) * P)
-                d = first_stage([(codes[:, m].bitcast(FP8X4), scales[:, m], v3, v3_sc)], nc.scalar.copy)
-                nc.vector.tensor_copy(xb[:, t, :], d[:].indirect(pos3_t[:]))
-            x.append(xb)
-            if b == 0:
-                w2_q = [quantize_dealt([w2_raw[0]], "w2q0")]
-
-        x_q = [quantize_plain(x[0], "xq0")]
-        w2_q.append(quantize_dealt([w2_raw[1]], "w2q1"))
+        x = [keep.tile([P, PACK, R], F32, name="x%d" % b) for b in range(2)]
+        az = [keep.tile([P, PACK, R], F32, name="az%d" % b, tag=("t3_win", "t2_win")[b], align_bytes=64) for b in range(2)]
         gate = keep.tile([P, N // P, R], F32, name="gate")
+        w4_q, x_q, z_q, picked = [], [], [], {}
+
+        def rows_d(i):
+            b, t = divmod(i, PACK)
+            codes, scales = w3_q[b]
+            m = slice(t * P, (t + 1) * P)
+            return first_stage([(codes[:, m].bitcast(FP8X4), scales[:, m], v3, v3_sc)], nc.scalar.copy)
+
+        def rows_fit(i):
+            b, t = divmod(i, PACK)
+            codes, scales = w2_q[b]
+            m = slice(t * P, (t + 1) * P)
+            return first_stage(
+                [(codes[:, m].bitcast(FP8X4), scales[:, m], v2, v2_sc)],
+                lambda dst, src: nc.scalar.activation(dst, src, ACT.Sigmoid, bias=b2_t[:, b, t : t + 1]),
+            )
+
+        def rows_a(i):
+            c0 = i * P
+            return first_stage(
+                [
+                    (w1_p[:, a, 2 * c0 : 2 * (c0 + P)].bitcast(FP4X4), w1_scale[a][:, c0 : c0 + P], v1[a], v1_scales[a])
+                    for a in range(2)
+                ],
+                nc.scalar.copy,
+            )
+
+        def pick_fit(i):
+            picked[i] = ring.tile([P, R], F32, name="picked_fit", bufs=4)
+            nc.vector.tensor_copy(picked[i][:], fit[i][:].indirect(pos2_t[:]))
 
         def gate_rows(u):
             bank = psum.tile([P, BANK], F32, name="bank")
@@ -209,48 +231,43 @@ def tile_list_costume_hire_features_kernel(
                 )
             nc.scalar.activation(gate[:, u, :], bank[:], ACT.Tanh, bias=b5_t[:, u : u + 1])
 
-        def pick_fit(i):
-            b, t = divmod(i, PACK)
-            codes, scales = w2_q[b]
-            m = slice(t * P, (t + 1) * P)
-            fit = first_stage(
-                [(codes[:, m].bitcast(FP8X4), scales[:, m], v2, v2_sc)],
-                lambda dst, src: nc.scalar.activation(dst, src, ACT.Sigmoid, bias=b2_t[:, b, t : t + 1]),
-            )
-            picked = ring.tile([P, R], F32, name="picked_fit", bufs=3)
-            nc.vector.tensor_copy(picked[:], fit[:].indirect(pos2_t[:]))
-            return picked
+        def first_z():
+            g = grouped_tile()
+            nc.vector.tensor_tensor(woven(g), planes(az[0]), planes(x[0]), ALU.subtract)
+            codes, scales = quantize(g, "zq0")
+            z_q.append([(codes[:, c0 : c0 + HALF], scales[:, c0 : c0 + HALF]) for c0 in (0, HALF)])
 
-        z_q = []
-        w4_q = []
-        az = [keep.tile([P, PACK, R], F32, name="az%d" % b, tag=("t3_win", "t2_win")[b], align_bytes=64) for b in range(2)]
-        picked_next = pick_fit(0)
+        def second_z():
+            halves = []
+            for h in range(2):
+                cols = slice(h * HALF, (h + 1) * HALF)
+                g = ring.tile([P, PACK * HALF], BF16, name="z_grouped", bufs=1, align_bytes=64)
+                nc.vector.tensor_tensor(woven(g), planes(az[1][:, :, cols]), planes(x[1][:, :, cols]), ALU.subtract)
+                halves.append(quantize(g, "zq1%d" % h))
+            z_q.append(halves)
+
         for i in range(2 * PACK):
             b, t = divmod(i, PACK)
-            picked_fit = picked_next
-            if i + 1 < 2 * PACK:
-                picked_next = pick_fit(i + 1)
-            c0 = i * P
-            a_rows = first_stage(
-                [
-                    (w1_p[:, a, 2 * c0 : 2 * (c0 + P)].bitcast(FP4X4), w1_scale[a][:, c0 : c0 + P], v1[a], v1_scales[a])
-                    for a in range(2)
-                ],
-                nc.scalar.copy,
-            )
-            nc.vector.tensor_tensor(az[b][:, t, :], a_rows[:].indirect(pos1_t[:]), picked_fit[:], ALU.mult)
+            nc.vector.tensor_copy(x[b][:, t, :], rows_d(i)[:].indirect(pos3_t[:]))
+        fit = [rows_fit(i) for i in range(PACK)]
+        late = grouped_tile()
+        w2_q.append(quantize_dealt([w2_raw[1]], "w2q1", late))
+        x_q.append(quantize_plain(x[0], "xq0", grouped_tile()))
+        for i in range(PACK):
+            pick_fit(i)
+        for i in range(2 * PACK):
+            b, t = divmod(i, PACK)
+            nc.vector.tensor_tensor(az[b][:, t, :], rows_a(i)[:].indirect(pos1_t[:]), picked[i][:], ALU.mult)
+            if 2 <= i < 2 + PACK:
+                fit.append(rows_fit(len(fit)))
+                pick_fit(len(fit) - 1)
             if i == 3:
-                x_q.append(quantize_plain(x[1], "xq1"))
+                x_q.append(quantize_plain(x[1], "xq1", late))
             if i in (5, 7):
-                w4_q.append(quantize_plain(w4_raw[len(w4_q)], "w4q%d" % len(w4_q)))
-            if t == PACK - 1:
-                halves = []
-                for h in range(2):
-                    cols = slice(h * HALF, (h + 1) * HALF)
-                    g = ring.tile([P, PACK * HALF], BF16, name="z_grouped", bufs=2, align_bytes=64)
-                    nc.vector.tensor_tensor(woven(g), planes(az[b][:, :, cols]), planes(x[b][:, :, cols]), ALU.subtract)
-                    halves.append(quantize(g, "zq%d%d" % (b, h)))
-                z_q.append(halves)
+                w4_q.append(quantize_plain(w4_raw[len(w4_q)], "w4q%d" % len(w4_q), grouped_tile()))
+            if i == 3:
+                first_z()
+        second_z()
 
         for u in range(N // P):
             gate_rows(u)

@@ -1,6 +1,7 @@
 from contextlib import ExitStack
 
 import concourse.mybir as mybir
+from concourse.masks import make_identity
 
 K, K2, T, S, R, H, N = 1024, 512, 2048, 1024, 512, 1024, 512
 FLOPS = 2 * (K * H * S + 2 * K2 * H * S + 2 * H * N * R)
@@ -21,6 +22,12 @@ PACK = 4
 PASS = P * PACK
 BANK = 512
 HALF = 256
+TILES = H // P
+LINE = 16
+
+FIRST_BUFS = TILES + PACK
+D_AHEAD = PACK + 2
+A_AHEAD = 2
 
 
 def tile_list_costume_hire_features_kernel(
@@ -35,93 +42,95 @@ def tile_list_costume_hire_features_kernel(
         psum = ctx.enter_context(tc.psum_pool(name="psum", bufs=8))
 
         def load_list(src, name):
-            t = lists.tile(list(src.shape), U16, name=name)
-            nc.sync.dma_start(t[:], src)
-            return t
+            offsets = lists.tile(list(src.shape), U16, name=name)
+            nc.sync.dma_start(offsets[:], src)
+            return offsets
 
         def zeroed_plane(width, name, engine):
-            t = keep.tile([P, width], U8, name=name, align_bytes=64)
-            engine.memset(t[:].bitcast(I32), 0)
-            return t
+            plane = keep.tile([P, width], U8, name=name, align_bytes=64)
+            engine.memset(plane[:].bitcast(I32), 0)
+            return plane
 
-        def load_table_scales(plane, scales):
+        def load_stacked_scales(plane, scales):
             passes = scales.shape[0]
             for q in range(4):
                 src = scales[:, 4 * q : 4 * q + 4, :] if passes > 1 else scales[0, 4 * q : 4 * q + 4, :]
                 nc.sync.dma_start(plane[32 * q : 32 * q + 4 * passes, :].bitcast(I32), src.bitcast(I32))
 
-        def load_weight_scales(plane, scales):
+        def load_adjacent_scales(plane, scales):
             for q in range(4):
                 nc.sync.dma_start(
-                    plane[32 * q : 32 * q + 4, :].rearrange("r (a c) -> r a c", a=2).bitcast(I32),
-                    scales[:, 4 * q : 4 * q + 4, :].rearrange("a r c -> r a c").bitcast(I32),
+                    plane[32 * q : 32 * q + 4, :].rearrange("s (g c) -> s g c", g=2).bitcast(I32),
+                    scales[:, 4 * q : 4 * q + 4, :].rearrange("g s c -> s g c").bitcast(I32),
                 )
 
-        def merged(words):
-            return words.rearrange("p t i -> p (t i)")
-
-        def load_words(rows, name):
-            t = keep.tile([P, rows.shape[1] // 4], I32, name=name, align_bytes=64)
-            nc.sync.dma_start(t[:], rows.bitcast(I32))
-            return t
+        def load_words(words, name):
+            window = keep.tile([P, words.shape[1]], I32, name=name, align_bytes=64)
+            nc.sync.dma_start(window[:], words.rearrange("p c t -> p (c t)").bitcast(I32))
+            return window
 
         def load_rows(rows, tag="raw", bufs=3):
             raw = ring.tile([P, PACK, rows.shape[1]], F32, name=tag, bufs=bufs)
-            nc.sync.dma_start(raw[:], rows.rearrange("(p j) c -> p j c", j=PACK))
+            nc.sync.dma_start(raw[:], rows.rearrange("(p t) c -> p t c", t=PACK))
             return raw
 
-        def gather_bytes(window, offsets, dtype, name, tag=None):
-            t = keep.tile([P, S], dtype, name=name, tag=tag or name, align_bytes=64)
-            nc.vector.tensor_copy(t[:], window[:].bitcast(dtype).indirect(offsets[:]))
-            return t
+        def gather_bytes(window, offsets, dtype, name):
+            picked_bytes = keep.tile([P, S], dtype, name=name, align_bytes=64)
+            nc.vector.tensor_copy(picked_bytes[:], window[:].bitcast(dtype).indirect(offsets[:]))
+            return picked_bytes
 
-        def grouped_tile():
-            return ring.tile([P, PACK * BANK], BF16, name="grouped", bufs=3, align_bytes=64)
+        def rounded_tile():
+            return ring.tile([P, PACK * BANK], BF16, name="rounded", bufs=3, align_bytes=64)
 
-        def quantize(g, name):
-            width = g.shape[1] // PACK
+        def quantize(rounded, name):
+            width = rounded.shape[1] // PACK
             codes = keep.tile([P, width], U32, name=name + "_codes", align_bytes=64)
             scales = keep.tile([P, width], U8, name=name + "_scales", align_bytes=64)
-            nc.vector.quantize_mx(out=codes[:].bitcast(FP8X4), scales=scales[:], in_=g[:])
+            nc.vector.quantize_mx(out=codes[:].bitcast(FP8X4), scales=scales[:], in_=rounded[:])
             return codes, scales
 
-        def quantize_dealt(parts, name, g):
-            dealt = g[:].rearrange("p (t m j) -> p m j t", t=PACK, j=PACK)
+        def quantize_dealt(parts, name, rounded):
+            dealt = rounded[:].rearrange("p (t m row) -> p m row t", t=PACK, row=PACK)
             m0 = 0
             for raw in parts:
                 m1 = m0 + raw.shape[2] // PACK
-                rows = raw[:].rearrange("p j (m t) -> p m j t", t=PACK)
+                source = raw[:].rearrange("p row (m t) -> p m row t", t=PACK)
                 for t0 in (0, 2):
-                    nc.scalar.copy(dealt[:, m0:m1, :, t0 : t0 + 2], rows[:, :, :, t0 : t0 + 2])
+                    nc.scalar.copy(dealt[:, m0:m1, :, t0 : t0 + 2], source[:, :, :, t0 : t0 + 2])
                 m0 = m1
-            return quantize(g, name)
+            return quantize(rounded, name)
 
-        def woven(g):
-            return g[:].rearrange("p (c i t) -> p c t i", i=2, t=PACK)
+        def woven(rounded):
+            return rounded[:].rearrange("p (c two t) -> p c t two", two=2, t=PACK)
 
-        def planes(raw):
-            return raw[:].rearrange("p t (c i) -> p c t i", i=2)
+        def rows_of(tile):
+            return tile[:].rearrange("p t (c two) -> p c t two", two=2)
 
-        def quantize_plain(raw, name, g):
-            nc.scalar.copy(woven(g), planes(raw))
-            return quantize(g, name)
+        def quantize_woven(tile, name, rounded):
+            nc.scalar.copy(woven(rounded), rows_of(tile))
+            return quantize(rounded, name)
+
+        first_banks = []
 
         def first_stage(operands, evacuate):
-            res = ring.tile([P, S], F32, name="first", bufs=12)
-            for h in range(S // BANK):
-                cols = slice(h * BANK, (h + 1) * BANK)
+            tile = ring.tile([P, S], F32, name="first", bufs=FIRST_BUFS)
+            for c0 in range(0, S, BANK):
+                cols = slice(c0, c0 + BANK)
                 bank = psum.tile([P, BANK], F32, name="bank")
-                for n, (lhs, lhs_scale, rhs, rhs_scale) in enumerate(operands):
+                first_banks.append(bank)
+                for step, (lhs, lhs_scale, rhs, rhs_scale) in enumerate(operands):
                     nc.tensor.matmul_mx(
                         out=bank[:], lhsT=lhs, lhsT_scale=lhs_scale, rhs=rhs[:, cols].bitcast(FP8X4),
-                        rhs_scale=rhs_scale[:, cols], start=(n == 0), stop=(n == len(operands) - 1),
+                        rhs_scale=rhs_scale[:, cols], start=(step == 0), stop=(step == len(operands) - 1),
                     )
-                evacuate(res[:, cols], bank[:])
-            return res
+                evacuate(tile[:, cols], bank[:])
+            return tile
 
-        s3_win = zeroed_plane(T, "s3_win", nc.gpsimd)
-        s2_win = zeroed_plane(T, "s2_win", nc.vector)
-        s1_win = zeroed_plane(T, "s1_win", nc.vector)
+        s3_window = zeroed_plane(T, "s3_window", nc.gpsimd)
+        identity = keep.tile([P, P], F32, name="identity")
+        make_identity(nc, identity[:])
+        s2_window = zeroed_plane(T, "s2_window", nc.vector)
+        s1_window = zeroed_plane(T, "s1_window", nc.vector)
         warm = keep.tile([P, 2], F32, name="warm")
         nc.vector.memset(warm[:, 0:1], 0.0)
         nc.scalar.activation(warm[:, 1:2], warm[:, 0:1], ACT.Sigmoid)
@@ -132,151 +141,205 @@ def tile_list_costume_hire_features_kernel(
 
         offs3_t = load_list(offs3, "offs3")
         offs2_t = load_list(offs2, "offs2")
-        w3_first = [load_rows(w3[:, 0:HALF], "raw_half", 2)]
-        load_table_scales(s3_win, tab3_scales)
-        t3_win = load_words(merged(tab3_words[0]), "t3_win")
-        w3_first.append(load_rows(w3[:, HALF:PASS], "raw_half", 2))
-        load_table_scales(s2_win, tab2_scales)
-        t2_win = load_words(merged(tab2_words[0]), "t2_win")
+        w3_first = [load_rows(w3[:, 0:HALF], "raw_part", 2)]
+        load_stacked_scales(s3_window, tab3_scales)
+        t3_window = load_words(tab3_words[0], "t3_window")
+        w3_first.append(load_rows(w3[:, HALF:PASS], "raw_part", 2))
+        load_stacked_scales(s2_window, tab2_scales)
+        t2_window = load_words(tab2_words[0], "t2_window")
         offs_t = load_list(offs, "offs")
-        load_table_scales(s1_win, tab_scales)
-        t1_win = [load_words(merged(tab_words[0]), "t1_win0")]
+        load_stacked_scales(s1_window, tab_scales)
+        t1_windows = [load_words(tab_words[0], "t1_window0")]
         w3_second = load_rows(w3[:, PASS : 2 * PASS])
-        w2_raw = [load_rows(w2[:, 0:PASS])]
+        w2_first = load_rows(w2[:, 0:PASS])
         b2_t = keep.tile([P, 2, PACK], F32, name="b2_t")
-        nc.sync.dma_start(b2_t[:], b2.rearrange("(b p t) -> p b t", b=2, t=PACK))
+        nc.sync.dma_start(b2_t[:], b2.rearrange("(g p t) -> p g t", g=2, t=PACK))
         w1_raw = keep.tile([P, 2, H // 2], I32, name="w1_raw", align_bytes=64)
-        nc.sync.dma_start(w1_raw[:], w1_words.rearrange("a p c -> p a c").bitcast(I32))
-        load_table_scales(w1_sc_raw, w1_scales)
-        t1_win.append(load_words(merged(tab_words[1]), "t1_win1"))
+        nc.sync.dma_start(w1_raw[:], w1_words.rearrange("kp p c -> p kp c").bitcast(I32))
+        load_stacked_scales(w1_sc_raw, w1_scales)
+        t1_windows.append(load_words(tab_words[1], "t1_window1"))
+        pos2_t = load_list(pos2, "pos2")
         pos3_t = load_list(pos3, "pos3")
-        pos1_t = load_list(pos1, "pos1")
 
-        v3_sc = gather_bytes(s3_win, offs3_t, U8, "v3_sc")
-        v3 = gather_bytes(t3_win, offs3_t, U32, "v3")
-        w3_q = [quantize_dealt(w3_first, "w3q0", grouped_tile())]
-        v2_sc = gather_bytes(s2_win, offs2_t, U8, "v2_sc")
-        v2 = gather_bytes(t2_win, offs2_t, U32, "v2")
-        v1_sc = gather_bytes(s1_win, offs_t, U8, "v1_sc")
-        v1 = [gather_bytes(t1_win[0], offs_t, U32, "v1_0")]
-        w3_q.append(quantize_dealt([w3_second], "w3q1", grouped_tile()))
-        w1_p = keep.tile([P, 2, 2 * H], U8, name="w1_p", align_bytes=64)
+        v3_sc = gather_bytes(s3_window, offs3_t, U8, "v3_sc")
+        v3 = gather_bytes(t3_window, offs3_t, U32, "v3")
+        w3_q = [quantize_dealt(w3_first, "w3q0", rounded_tile())]
+        v2_sc = gather_bytes(s2_window, offs2_t, U8, "v2_sc")
+        v2 = gather_bytes(t2_window, offs2_t, U32, "v2")
+        v1_sc = gather_bytes(s1_window, offs_t, U8, "v1_sc")
+        v1 = [gather_bytes(t1_windows[0], offs_t, U32, "v1_0")]
+        w3_q.append(quantize_dealt([w3_second], "w3q1", rounded_tile()))
+        w1_dealt = keep.tile([P, 2, 2 * H], U8, name="w1_dealt", align_bytes=64)
         nc.vector.tensor_copy(
-            w1_p[:].bitcast(U16).rearrange("p a (b t g m) -> p (a b) g t m", b=2, t=PACK, m=8),
-            w1_raw[:].bitcast(U16).rearrange("p a (b g m t) -> p (a b) g t m", b=2, t=PACK, m=8),
+            w1_dealt[:].bitcast(U16).rearrange("p kp (g t l m) -> p (kp g) l t m", g=2, t=PACK, m=LINE // 2),
+            w1_raw[:].bitcast(U16).rearrange("p kp (g l m t) -> p (kp g) l t m", g=2, t=PACK, m=LINE // 2),
         )
-        w2_q = [quantize_dealt([w2_raw[0]], "w2q0", grouped_tile())]
+        w2_q = [quantize_dealt([w2_first], "w2q0", rounded_tile())]
         w1_sc = keep.tile([P, H], U8, name="w1_sc", align_bytes=64)
         nc.vector.tensor_copy(
-            w1_sc[:].rearrange("p (b t g m) -> p b g t m", b=2, t=PACK, m=16),
-            w1_sc_raw[:].rearrange("p (b g m t) -> p b g t m", b=2, t=PACK, m=16),
+            w1_sc[:].rearrange("p (g t l m) -> p g l t m", g=2, t=PACK, m=LINE),
+            w1_sc_raw[:].rearrange("p (g l m t) -> p g l t m", g=2, t=PACK, m=LINE),
         )
-        v1.append(gather_bytes(t1_win[1], offs_t, U32, "v1_1"))
-        w1_scale = [w1_sc, w1_sc_pass1]
-        v1_scales = [v1_sc, v1_sc_pass1]
+        v1.append(gather_bytes(t1_windows[1], offs_t, U32, "v1_1"))
+        w1_planes = [w1_sc, w1_sc_pass1]
+        v1_planes = [v1_sc, v1_sc_pass1]
         nc.sync.dma_start(v1_sc_pass1[0:112, :].bitcast(I32), v1_sc[4:116, :].bitcast(I32))
-        w2_raw.append(load_rows(w2[:, PASS : 2 * PASS]))
+        w2_second = load_rows(w2[:, PASS : 2 * PASS])
         nc.sync.dma_start(w1_sc_pass1[0:112, :].bitcast(I32), w1_sc[4:116, :].bitcast(I32))
         w4_raw = [load_rows(w4[0:PASS, :])]
-        pos2_t = load_list(pos2, "pos2")
+        pos1_t = load_list(pos1, "pos1")
         w5_w = keep.tile([P, 2, N], I32, name="w5_w", align_bytes=64)
-        nc.sync.dma_start(w5_w[:], w5_words.rearrange("a p c i -> p a (c i)").bitcast(I32))
-        load_weight_scales(w5_sc, w5_scales)
+        nc.sync.dma_start(w5_w[:], w5_words.rearrange("g p c t -> p g (c t)").bitcast(I32))
+        load_adjacent_scales(w5_sc, w5_scales)
         w4_raw.append(load_rows(w4[PASS : 2 * PASS, :]))
         b5_t = keep.tile([P, N // P], F32, name="b5_t")
         with nc.allow_non_contiguous_dma(reason="one bias value a partition and output tile"):
             nc.sync.dma_start(b5_t[:], b5.rearrange("(u p) -> p u", p=P))
 
-        x = [keep.tile([P, PACK, R], F32, name="x%d" % b) for b in range(2)]
-        az = [keep.tile([P, PACK, R], F32, name="az%d" % b, tag=("t3_win", "t2_win")[b], align_bytes=64) for b in range(2)]
+        fit_first = keep.tile([P, PACK, R], F32, name="fit_first")
+        x = [keep.tile([P, PACK, R], F32, name="x%d" % g, tag=("x0", "fit_first")[g]) for g in range(2)]
+        product = [
+            keep.tile([P, PACK, R], F32, name="product%d" % g, tag=("t3_window", "t2_window")[g], align_bytes=64)
+            for g in range(2)
+        ]
         gate = keep.tile([P, N // P, R], F32, name="gate")
-        w4_q, x_q, z_q, picked = [], [], [], {}
 
-        def rows_d(i):
-            b, t = divmod(i, PACK)
-            codes, scales = w3_q[b]
-            m = slice(t * P, (t + 1) * P)
-            return first_stage([(codes[:, m].bitcast(FP8X4), scales[:, m], v3, v3_sc)], nc.scalar.copy)
+        def tile_of_d(i):
+            g, t = divmod(i, PACK)
+            codes, scales = w3_q[g]
+            rows = slice(t * P, (t + 1) * P)
+            return first_stage([(codes[:, rows].bitcast(FP8X4), scales[:, rows], v3, v3_sc)], nc.scalar.copy)
 
-        def rows_fit(i):
-            b, t = divmod(i, PACK)
-            codes, scales = w2_q[b]
-            m = slice(t * P, (t + 1) * P)
+        def tile_of_fit(i):
+            g, t = divmod(i, PACK)
+            codes, scales = w2_q[g]
+            rows = slice(t * P, (t + 1) * P)
             return first_stage(
-                [(codes[:, m].bitcast(FP8X4), scales[:, m], v2, v2_sc)],
-                lambda dst, src: nc.scalar.activation(dst, src, ACT.Sigmoid, bias=b2_t[:, b, t : t + 1]),
+                [(codes[:, rows].bitcast(FP8X4), scales[:, rows], v2, v2_sc)],
+                lambda dst, src: nc.scalar.activation(dst, src, ACT.Sigmoid, bias=b2_t[:, g, t : t + 1]),
             )
 
-        def rows_a(i):
+        def tile_of_a(i):
             c0 = i * P
             return first_stage(
                 [
-                    (w1_p[:, a, 2 * c0 : 2 * (c0 + P)].bitcast(FP4X4), w1_scale[a][:, c0 : c0 + P], v1[a], v1_scales[a])
-                    for a in range(2)
+                    (
+                        w1_dealt[:, kp, 2 * c0 : 2 * (c0 + P)].bitcast(FP4X4), w1_planes[kp][:, c0 : c0 + P],
+                        v1[kp], v1_planes[kp],
+                    )
+                    for kp in range(2)
                 ],
-                nc.scalar.copy,
+                nc.scalar.copy if i >= PACK else lambda dst, src: nc.scalar.mul(dst, src, -1.0),
             )
 
+        d_tiles, fit_tiles, a_tiles, picked_fit = [], [], [], []
+
         def pick_fit(i):
-            picked[i] = ring.tile([P, R], F32, name="picked_fit", bufs=4)
-            nc.vector.tensor_copy(picked[i][:], fit[i][:].indirect(pos2_t[:]))
+            dst = fit_first[:, i, :] if i < PACK else ring.tile([P, R], F32, name="picked_fit", bufs=3)[:]
+            nc.vector.tensor_copy(dst, fit_tiles[i][:].indirect(pos2_t[:]))
+            picked_fit.append(dst)
 
-        def gate_rows(u):
-            bank = psum.tile([P, BANK], F32, name="bank")
-            for a in range(2):
-                nc.tensor.matmul_mx(
-                    out=bank[:], lhsT=w5_w[:, a, u * P : (u + 1) * P].bitcast(FP8X4),
-                    lhsT_scale=w5_sc[:, a * N + u * P : a * N + (u + 1) * P],
-                    rhs=x_q[a][0][:].bitcast(FP8X4), rhs_scale=x_q[a][1][:], start=(a == 0), stop=(a == 1),
-                )
-            nc.scalar.activation(gate[:, u, :], bank[:], ACT.Tanh, bias=b5_t[:, u : u + 1])
+        def pick_x(i):
+            g, t = divmod(i, PACK)
+            nc.vector.tensor_copy(x[g][:, t, :], d_tiles[i][:].indirect(pos3_t[:]))
 
-        def first_z():
-            g = grouped_tile()
-            nc.vector.tensor_tensor(woven(g), planes(az[0]), planes(x[0]), ALU.subtract)
-            codes, scales = quantize(g, "zq0")
-            z_q.append([(codes[:, c0 : c0 + HALF], scales[:, c0 : c0 + HALF]) for c0 in (0, HALF)])
+        def pick_product(i):
+            g, t = divmod(i, PACK)
+            nc.vector.tensor_tensor(product[g][:, t, :], a_tiles[i][:].indirect(pos1_t[:]), picked_fit[i], ALU.mult)
 
-        def second_z():
+        def first_half_of_z(banks):
+            rounded = rounded_tile()
+            words = rounded[:].bitcast(F32).rearrange("p (j w) -> p j w", w=2)
+            for h in range(2):
+                turned = []
+                for group in (2 * h, 2 * h + 1):
+                    cols = slice(group * P, (group + 1) * P)
+                    bank = banks[group][:].rearrange("j (t p) -> j t p", t=PACK)
+                    for t in range(PACK):
+                        for src, opens in ((x[0], True), (product[0], False)):
+                            nc.tensor.matmul(
+                                bank[:, t, :], src[:, t, cols], identity[:],
+                                start=opens, stop=not opens, is_transpose=True,
+                            )
+                    z_turned = ring.tile([P, PASS], BF16, name="z_turned", bufs=R // P)
+                    nc.scalar.mul(
+                        z_turned[:].rearrange("j (w p e) -> j w p e", w=2, e=2),
+                        bank.rearrange("j (w e) p -> j w p e", e=2), -1.0,
+                    )
+                    turned.append(z_turned)
+                back = banks[2 * h][:].rearrange("p (w j) -> p w j", w=2)
+                for side in range(2):
+                    for w in range(2):
+                        nc.tensor.transpose(
+                            back[:, w, side * P : (side + 1) * P],
+                            turned[side][:].bitcast(F32)[:, w * P : (w + 1) * P], identity[:],
+                        )
+                nc.scalar.copy(words[:, h * HALF : (h + 1) * HALF, :], back.rearrange("p w j -> p j w"))
+            codes, scales = quantize(rounded, "zq0")
+            return [(codes[:, c0 : c0 + HALF], scales[:, c0 : c0 + HALF]) for c0 in (0, HALF)]
+
+        def second_half_of_z(rounded):
             halves = []
             for h in range(2):
                 cols = slice(h * HALF, (h + 1) * HALF)
-                g = ring.tile([P, PACK * HALF], BF16, name="z_grouped", bufs=1, align_bytes=64)
-                nc.vector.tensor_tensor(woven(g), planes(az[1][:, :, cols]), planes(x[1][:, :, cols]), ALU.subtract)
-                halves.append(quantize(g, "zq1%d" % h))
-            z_q.append(halves)
+                part = rounded[:, h * PACK * HALF : (h + 1) * PACK * HALF]
+                nc.vector.tensor_tensor(
+                    woven(part), rows_of(product[1][:, :, cols]), rows_of(x[1][:, :, cols]), ALU.subtract
+                )
+                halves.append(quantize(part, "zq1%d" % h))
+            return halves
 
-        for i in range(2 * PACK):
-            b, t = divmod(i, PACK)
-            nc.vector.tensor_copy(x[b][:, t, :], rows_d(i)[:].indirect(pos3_t[:]))
-        fit = [rows_fit(i) for i in range(PACK)]
-        late = grouped_tile()
-        w2_q.append(quantize_dealt([w2_raw[1]], "w2q1", late))
-        x_q.append(quantize_plain(x[0], "xq0", grouped_tile()))
+        d_tiles.extend([tile_of_d(i) for i in range(D_AHEAD)])
+        fit_tiles.extend([tile_of_fit(i) for i in range(PACK)])
         for i in range(PACK):
             pick_fit(i)
-        for i in range(2 * PACK):
-            b, t = divmod(i, PACK)
-            nc.vector.tensor_tensor(az[b][:, t, :], rows_a(i)[:].indirect(pos1_t[:]), picked[i][:], ALU.mult)
-            if 2 <= i < 2 + PACK:
-                fit.append(rows_fit(len(fit)))
-                pick_fit(len(fit) - 1)
-            if i == 3:
-                x_q.append(quantize_plain(x[1], "xq1", late))
-            if i in (5, 7):
-                w4_q.append(quantize_plain(w4_raw[len(w4_q)], "w4q%d" % len(w4_q), grouped_tile()))
-            if i == 3:
-                first_z()
-        second_z()
+        for i in range(PACK):
+            pick_x(i)
+        d_tiles.extend([tile_of_d(i) for i in range(D_AHEAD, TILES)])
+        a_tiles.extend([tile_of_a(i) for i in range(A_AHEAD)])
+        rounded_second = rounded_tile()
+        w2_q.append(quantize_dealt([w2_second], "w2q1", rounded_second))
+        a_tiles.extend([tile_of_a(i) for i in range(A_AHEAD, PACK)])
+        for i in range(PACK):
+            pick_product(i)
+        x_q = [quantize_woven(x[0], "xq0", rounded_tile())]
+
+        fit_tiles.extend([tile_of_fit(i) for i in range(PACK, PACK + 2)])
+        z_banks = first_banks[-(R // P) :]
+        a_tiles.append(tile_of_a(PACK))
+        w4_q = [quantize_woven(w4_raw[0], "w4q0", rounded_tile())]
+        z_q = [first_half_of_z(z_banks)]
+
+        for i in range(PACK, TILES):
+            pick_x(i)
+        pick_fit(PACK)
+        pick_fit(PACK + 1)
+        pick_product(PACK)
+        for i in range(PACK + 1, TILES):
+            if i + 1 < TILES:
+                fit_tiles.append(tile_of_fit(i + 1))
+                pick_fit(i + 1)
+            a_tiles.append(tile_of_a(i))
+            pick_product(i)
+        x_q.append(quantize_woven(x[1], "xq1", rounded_second))
+        w4_q.append(quantize_woven(w4_raw[1], "w4q1", rounded_tile()))
+        z_q.append(second_half_of_z(rounded_second))
 
         for u in range(N // P):
-            gate_rows(u)
+            bank = psum.tile([P, BANK], F32, name="bank")
+            for g in range(2):
+                nc.tensor.matmul_mx(
+                    out=bank[:], lhsT=w5_w[:, g, u * P : (u + 1) * P].bitcast(FP8X4),
+                    lhsT_scale=w5_sc[:, g * N + u * P : g * N + (u + 1) * P],
+                    rhs=x_q[g][0][:].bitcast(FP8X4), rhs_scale=x_q[g][1][:], start=(g == 0), stop=(g == 1),
+                )
+            nc.scalar.activation(gate[:, u, :], bank[:], ACT.Tanh, bias=b5_t[:, u : u + 1])
 
-        def y_pass(bank, u, h, a):
-            m = slice(u * P, (u + 1) * P)
+        def y_pass(bank, u, h, g):
+            rows = slice(u * P, (u + 1) * P)
             nc.tensor.matmul_mx(
-                out=bank[:], lhsT=w4_q[a][0][:, m].bitcast(FP8X4), lhsT_scale=w4_q[a][1][:, m],
-                rhs=z_q[a][h][0][:].bitcast(FP8X4), rhs_scale=z_q[a][h][1][:], start=(a == 0), stop=(a == 1),
+                out=bank[:], lhsT=w4_q[g][0][:, rows].bitcast(FP8X4), lhsT_scale=w4_q[g][1][:, rows],
+                rhs=z_q[g][h][0][:].bitcast(FP8X4), rhs_scale=z_q[g][h][1][:], start=(g == 0), stop=(g == 1),
             )
 
         y = {}
@@ -287,10 +350,10 @@ def tile_list_costume_hire_features_kernel(
         for h in range(2):
             cols = slice(h * HALF, (h + 1) * HALF)
             for pair in range(2):
-                res = ring.tile([P, 2, HALF], F32, name="res", bufs=4)
-                for i in range(2):
-                    u = 2 * pair + i
+                result = ring.tile([P, 2, HALF], F32, name="result", bufs=4)
+                for side in range(2):
+                    u = 2 * pair + side
                     y_pass(y[h, u], u, h, 1)
-                    nc.vector.tensor_tensor(res[:, i, :], y[h, u][:], gate[:, u, cols], ALU.mult)
-                rows = out[2 * pair * P : 2 * (pair + 1) * P, cols]
-                nc.sync.dma_start(rows.rearrange("(i p) j -> p i j", p=P), res[:])
+                    nc.vector.tensor_tensor(result[:, side, :], y[h, u][:], gate[:, u, cols], ALU.mult)
+                stored = out[2 * pair * P : 2 * (pair + 1) * P, cols]
+                nc.sync.dma_start(stored.rearrange("(side p) j -> p side j", p=P), result[:])

from contextlib import ExitStack

import concourse.mybir as mybir
from concourse.masks import make_identity

K, K2, T, S, R, H, N = 1024, 512, 2048, 1024, 512, 1024, 512
FLOPS = 2 * (K * H * S + 2 * K2 * H * S + 2 * H * N * R)

F32 = mybir.dt.float32
BF16 = mybir.dt.bfloat16
I32 = mybir.dt.int32
U32 = mybir.dt.uint32
U16 = mybir.dt.uint16
U8 = mybir.dt.uint8
FP8X4 = mybir.dt.float8_e4m3fn_x4
FP4X4 = mybir.dt.float4_e2m1fn_x4
ACT = mybir.ActivationFunctionType
ALU = mybir.AluOpType

P = 128
PACK = 4
PASS = P * PACK
BANK = 512
HALF = 256
TILES = H // P
LINE = 16

FIRST_BUFS = TILES + PACK
D_AHEAD = PACK + 2
A_AHEAD = 2


def tile_list_costume_hire_features_kernel(
    tc, tab_words, tab_scales, tab2_words, tab2_scales, tab3_words, tab3_scales, offs, offs2, offs3,
    pos1, pos2, pos3, w1_words, w1_scales, w2, b2, w3, w4, w5_words, w5_scales, b5, out,
):
    nc = tc.nc
    with ExitStack() as ctx:
        lists = ctx.enter_context(tc.tile_pool(name="lists", bufs=1))
        keep = ctx.enter_context(tc.tile_pool(name="keep", bufs=1))
        ring = ctx.enter_context(tc.tile_pool(name="ring", bufs=1))
        psum = ctx.enter_context(tc.psum_pool(name="psum", bufs=8))

        def load_list(src, name):
            offsets = lists.tile(list(src.shape), U16, name=name)
            nc.sync.dma_start(offsets[:], src)
            return offsets

        def zeroed_plane(width, name, engine):
            plane = keep.tile([P, width], U8, name=name, align_bytes=64)
            engine.memset(plane[:].bitcast(I32), 0)
            return plane

        def load_stacked_scales(plane, scales):
            passes = scales.shape[0]
            for q in range(4):
                src = scales[:, 4 * q : 4 * q + 4, :] if passes > 1 else scales[0, 4 * q : 4 * q + 4, :]
                nc.sync.dma_start(plane[32 * q : 32 * q + 4 * passes, :].bitcast(I32), src.bitcast(I32))

        def load_adjacent_scales(plane, scales):
            for q in range(4):
                nc.sync.dma_start(
                    plane[32 * q : 32 * q + 4, :].rearrange("s (g c) -> s g c", g=2).bitcast(I32),
                    scales[:, 4 * q : 4 * q + 4, :].rearrange("g s c -> s g c").bitcast(I32),
                )

        def load_words(words, name):
            window = keep.tile([P, words.shape[1]], I32, name=name, align_bytes=64)
            nc.sync.dma_start(window[:], words.rearrange("p c t -> p (c t)").bitcast(I32))
            return window

        def load_rows(rows, tag="raw", bufs=3):
            raw = ring.tile([P, PACK, rows.shape[1]], F32, name=tag, bufs=bufs)
            nc.sync.dma_start(raw[:], rows.rearrange("(p t) c -> p t c", t=PACK))
            return raw

        def gather_bytes(window, offsets, dtype, name):
            picked_bytes = keep.tile([P, S], dtype, name=name, align_bytes=64)
            nc.vector.tensor_copy(picked_bytes[:], window[:].bitcast(dtype).indirect(offsets[:]))
            return picked_bytes

        def rounded_tile():
            return ring.tile([P, PACK * BANK], BF16, name="rounded", bufs=3, align_bytes=64)

        def quantize(rounded, name):
            width = rounded.shape[1] // PACK
            codes = keep.tile([P, width], U32, name=name + "_codes", align_bytes=64)
            scales = keep.tile([P, width], U8, name=name + "_scales", align_bytes=64)
            nc.vector.quantize_mx(out=codes[:].bitcast(FP8X4), scales=scales[:], in_=rounded[:])
            return codes, scales

        def quantize_dealt(parts, name, rounded):
            dealt = rounded[:].rearrange("p (t m row) -> p m row t", t=PACK, row=PACK)
            m0 = 0
            for raw in parts:
                m1 = m0 + raw.shape[2] // PACK
                source = raw[:].rearrange("p row (m t) -> p m row t", t=PACK)
                for t0 in (0, 2):
                    nc.scalar.copy(dealt[:, m0:m1, :, t0 : t0 + 2], source[:, :, :, t0 : t0 + 2])
                m0 = m1
            return quantize(rounded, name)

        def woven(rounded):
            return rounded[:].rearrange("p (c two t) -> p c t two", two=2, t=PACK)

        def rows_of(tile):
            return tile[:].rearrange("p t (c two) -> p c t two", two=2)

        def quantize_woven(tile, name, rounded):
            nc.scalar.copy(woven(rounded), rows_of(tile))
            return quantize(rounded, name)

        first_banks = []

        def first_stage(operands, evacuate):
            tile = ring.tile([P, S], F32, name="first", bufs=FIRST_BUFS)
            for c0 in range(0, S, BANK):
                cols = slice(c0, c0 + BANK)
                bank = psum.tile([P, BANK], F32, name="bank")
                first_banks.append(bank)
                for step, (lhs, lhs_scale, rhs, rhs_scale) in enumerate(operands):
                    nc.tensor.matmul_mx(
                        out=bank[:], lhsT=lhs, lhsT_scale=lhs_scale, rhs=rhs[:, cols].bitcast(FP8X4),
                        rhs_scale=rhs_scale[:, cols], start=(step == 0), stop=(step == len(operands) - 1),
                    )
                evacuate(tile[:, cols], bank[:])
            return tile

        s3_window = zeroed_plane(T, "s3_window", nc.gpsimd)
        identity = keep.tile([P, P], F32, name="identity")
        make_identity(nc, identity[:])
        s2_window = zeroed_plane(T, "s2_window", nc.vector)
        s1_window = zeroed_plane(T, "s1_window", nc.vector)
        warm = keep.tile([P, 2], F32, name="warm")
        nc.vector.memset(warm[:, 0:1], 0.0)
        nc.scalar.activation(warm[:, 1:2], warm[:, 0:1], ACT.Sigmoid)
        w1_sc_raw = zeroed_plane(H, "w1_sc_raw", nc.vector)
        w1_sc_pass1 = zeroed_plane(H, "w1_sc_pass1", nc.vector)
        v1_sc_pass1 = zeroed_plane(S, "v1_sc_pass1", nc.vector)
        w5_sc = zeroed_plane(2 * N, "w5_sc", nc.vector)

        offs3_t = load_list(offs3, "offs3")
        offs2_t = load_list(offs2, "offs2")
        w3_first = [load_rows(w3[:, 0:HALF], "raw_part", 2)]
        load_stacked_scales(s3_window, tab3_scales)
        t3_window = load_words(tab3_words[0], "t3_window")
        w3_first.append(load_rows(w3[:, HALF:PASS], "raw_part", 2))
        load_stacked_scales(s2_window, tab2_scales)
        t2_window = load_words(tab2_words[0], "t2_window")
        offs_t = load_list(offs, "offs")
        load_stacked_scales(s1_window, tab_scales)
        t1_windows = [load_words(tab_words[0], "t1_window0")]
        w3_second = load_rows(w3[:, PASS : 2 * PASS])
        w2_first = load_rows(w2[:, 0:PASS])
        b2_t = keep.tile([P, 2, PACK], F32, name="b2_t")
        nc.sync.dma_start(b2_t[:], b2.rearrange("(g p t) -> p g t", g=2, t=PACK))
        w1_raw = keep.tile([P, 2, H // 2], I32, name="w1_raw", align_bytes=64)
        nc.sync.dma_start(w1_raw[:], w1_words.rearrange("kp p c -> p kp c").bitcast(I32))
        load_stacked_scales(w1_sc_raw, w1_scales)
        t1_windows.append(load_words(tab_words[1], "t1_window1"))
        pos2_t = load_list(pos2, "pos2")
        pos3_t = load_list(pos3, "pos3")

        v3_sc = gather_bytes(s3_window, offs3_t, U8, "v3_sc")
        v3 = gather_bytes(t3_window, offs3_t, U32, "v3")
        w3_q = [quantize_dealt(w3_first, "w3q0", rounded_tile())]
        v2_sc = gather_bytes(s2_window, offs2_t, U8, "v2_sc")
        v2 = gather_bytes(t2_window, offs2_t, U32, "v2")
        v1_sc = gather_bytes(s1_window, offs_t, U8, "v1_sc")
        v1 = [gather_bytes(t1_windows[0], offs_t, U32, "v1_0")]
        w3_q.append(quantize_dealt([w3_second], "w3q1", rounded_tile()))
        w1_dealt = keep.tile([P, 2, 2 * H], U8, name="w1_dealt", align_bytes=64)
        nc.vector.tensor_copy(
            w1_dealt[:].bitcast(U16).rearrange("p kp (g t l m) -> p (kp g) l t m", g=2, t=PACK, m=LINE // 2),
            w1_raw[:].bitcast(U16).rearrange("p kp (g l m t) -> p (kp g) l t m", g=2, t=PACK, m=LINE // 2),
        )
        w2_q = [quantize_dealt([w2_first], "w2q0", rounded_tile())]
        w1_sc = keep.tile([P, H], U8, name="w1_sc", align_bytes=64)
        nc.vector.tensor_copy(
            w1_sc[:].rearrange("p (g t l m) -> p g l t m", g=2, t=PACK, m=LINE),
            w1_sc_raw[:].rearrange("p (g l m t) -> p g l t m", g=2, t=PACK, m=LINE),
        )
        v1.append(gather_bytes(t1_windows[1], offs_t, U32, "v1_1"))
        w1_planes = [w1_sc, w1_sc_pass1]
        v1_planes = [v1_sc, v1_sc_pass1]
        nc.sync.dma_start(v1_sc_pass1[0:112, :].bitcast(I32), v1_sc[4:116, :].bitcast(I32))
        w2_second = load_rows(w2[:, PASS : 2 * PASS])
        nc.sync.dma_start(w1_sc_pass1[0:112, :].bitcast(I32), w1_sc[4:116, :].bitcast(I32))
        w4_raw = [load_rows(w4[0:PASS, :])]
        pos1_t = load_list(pos1, "pos1")
        w5_w = keep.tile([P, 2, N], I32, name="w5_w", align_bytes=64)
        nc.sync.dma_start(w5_w[:], w5_words.rearrange("g p c t -> p g (c t)").bitcast(I32))
        load_adjacent_scales(w5_sc, w5_scales)
        w4_raw.append(load_rows(w4[PASS : 2 * PASS, :]))
        b5_t = keep.tile([P, N // P], F32, name="b5_t")
        with nc.allow_non_contiguous_dma(reason="one bias value a partition and output tile"):
            nc.sync.dma_start(b5_t[:], b5.rearrange("(u p) -> p u", p=P))

        fit_first = keep.tile([P, PACK, R], F32, name="fit_first")
        x = [keep.tile([P, PACK, R], F32, name="x%d" % g, tag=("x0", "fit_first")[g]) for g in range(2)]
        product = [
            keep.tile([P, PACK, R], F32, name="product%d" % g, tag=("t3_window", "t2_window")[g], align_bytes=64)
            for g in range(2)
        ]
        gate = keep.tile([P, N // P, R], F32, name="gate")

        def tile_of_d(i):
            g, t = divmod(i, PACK)
            codes, scales = w3_q[g]
            rows = slice(t * P, (t + 1) * P)
            return first_stage([(codes[:, rows].bitcast(FP8X4), scales[:, rows], v3, v3_sc)], nc.scalar.copy)

        def tile_of_fit(i):
            g, t = divmod(i, PACK)
            codes, scales = w2_q[g]
            rows = slice(t * P, (t + 1) * P)
            return first_stage(
                [(codes[:, rows].bitcast(FP8X4), scales[:, rows], v2, v2_sc)],
                lambda dst, src: nc.scalar.activation(dst, src, ACT.Sigmoid, bias=b2_t[:, g, t : t + 1]),
            )

        def tile_of_a(i):
            c0 = i * P
            return first_stage(
                [
                    (
                        w1_dealt[:, kp, 2 * c0 : 2 * (c0 + P)].bitcast(FP4X4), w1_planes[kp][:, c0 : c0 + P],
                        v1[kp], v1_planes[kp],
                    )
                    for kp in range(2)
                ],
                nc.scalar.copy if i >= PACK else lambda dst, src: nc.scalar.mul(dst, src, -1.0),
            )

        d_tiles, fit_tiles, a_tiles, picked_fit = [], [], [], []

        def pick_fit(i):
            dst = fit_first[:, i, :] if i < PACK else ring.tile([P, R], F32, name="picked_fit", bufs=3)[:]
            nc.vector.tensor_copy(dst, fit_tiles[i][:].indirect(pos2_t[:]))
            picked_fit.append(dst)

        def pick_x(i):
            g, t = divmod(i, PACK)
            nc.vector.tensor_copy(x[g][:, t, :], d_tiles[i][:].indirect(pos3_t[:]))

        def pick_product(i):
            g, t = divmod(i, PACK)
            nc.vector.tensor_tensor(product[g][:, t, :], a_tiles[i][:].indirect(pos1_t[:]), picked_fit[i], ALU.mult)

        def first_half_of_z(banks):
            rounded = rounded_tile()
            words = rounded[:].bitcast(F32).rearrange("p (j w) -> p j w", w=2)
            for h in range(2):
                turned = []
                for group in (2 * h, 2 * h + 1):
                    cols = slice(group * P, (group + 1) * P)
                    bank = banks[group][:].rearrange("j (t p) -> j t p", t=PACK)
                    for t in range(PACK):
                        for src, opens in ((x[0], True), (product[0], False)):
                            nc.tensor.matmul(
                                bank[:, t, :], src[:, t, cols], identity[:],
                                start=opens, stop=not opens, is_transpose=True,
                            )
                    z_turned = ring.tile([P, PASS], BF16, name="z_turned", bufs=R // P)
                    nc.scalar.mul(
                        z_turned[:].rearrange("j (w p e) -> j w p e", w=2, e=2),
                        bank.rearrange("j (w e) p -> j w p e", e=2), -1.0,
                    )
                    turned.append(z_turned)
                back = banks[2 * h][:].rearrange("p (w j) -> p w j", w=2)
                for side in range(2):
                    for w in range(2):
                        nc.tensor.transpose(
                            back[:, w, side * P : (side + 1) * P],
                            turned[side][:].bitcast(F32)[:, w * P : (w + 1) * P], identity[:],
                        )
                nc.scalar.copy(words[:, h * HALF : (h + 1) * HALF, :], back.rearrange("p w j -> p j w"))
            codes, scales = quantize(rounded, "zq0")
            return [(codes[:, c0 : c0 + HALF], scales[:, c0 : c0 + HALF]) for c0 in (0, HALF)]

        def second_half_of_z(rounded):
            halves = []
            for h in range(2):
                cols = slice(h * HALF, (h + 1) * HALF)
                part = rounded[:, h * PACK * HALF : (h + 1) * PACK * HALF]
                nc.vector.tensor_tensor(
                    woven(part), rows_of(product[1][:, :, cols]), rows_of(x[1][:, :, cols]), ALU.subtract
                )
                halves.append(quantize(part, "zq1%d" % h))
            return halves

        d_tiles.extend([tile_of_d(i) for i in range(D_AHEAD)])
        fit_tiles.extend([tile_of_fit(i) for i in range(PACK)])
        for i in range(PACK):
            pick_fit(i)
        for i in range(PACK):
            pick_x(i)
        d_tiles.extend([tile_of_d(i) for i in range(D_AHEAD, TILES)])
        a_tiles.extend([tile_of_a(i) for i in range(A_AHEAD)])
        rounded_second = rounded_tile()
        w2_q.append(quantize_dealt([w2_second], "w2q1", rounded_second))
        a_tiles.extend([tile_of_a(i) for i in range(A_AHEAD, PACK)])
        for i in range(PACK):
            pick_product(i)
        x_q = [quantize_woven(x[0], "xq0", rounded_tile())]

        fit_tiles.extend([tile_of_fit(i) for i in range(PACK, PACK + 2)])
        z_banks = first_banks[-(R // P) :]
        a_tiles.append(tile_of_a(PACK))
        w4_q = [quantize_woven(w4_raw[0], "w4q0", rounded_tile())]
        z_q = [first_half_of_z(z_banks)]

        for i in range(PACK, TILES):
            pick_x(i)
        pick_fit(PACK)
        pick_fit(PACK + 1)
        pick_product(PACK)
        for i in range(PACK + 1, TILES):
            if i + 1 < TILES:
                fit_tiles.append(tile_of_fit(i + 1))
                pick_fit(i + 1)
            a_tiles.append(tile_of_a(i))
            pick_product(i)
        x_q.append(quantize_woven(x[1], "xq1", rounded_second))
        w4_q.append(quantize_woven(w4_raw[1], "w4q1", rounded_tile()))
        z_q.append(second_half_of_z(rounded_second))

        for u in range(N // P):
            bank = psum.tile([P, BANK], F32, name="bank")
            for g in range(2):
                nc.tensor.matmul_mx(
                    out=bank[:], lhsT=w5_w[:, g, u * P : (u + 1) * P].bitcast(FP8X4),
                    lhsT_scale=w5_sc[:, g * N + u * P : g * N + (u + 1) * P],
                    rhs=x_q[g][0][:].bitcast(FP8X4), rhs_scale=x_q[g][1][:], start=(g == 0), stop=(g == 1),
                )
            nc.scalar.activation(gate[:, u, :], bank[:], ACT.Tanh, bias=b5_t[:, u : u + 1])

        def y_pass(bank, u, h, g):
            rows = slice(u * P, (u + 1) * P)
            nc.tensor.matmul_mx(
                out=bank[:], lhsT=w4_q[g][0][:, rows].bitcast(FP8X4), lhsT_scale=w4_q[g][1][:, rows],
                rhs=z_q[g][h][0][:].bitcast(FP8X4), rhs_scale=z_q[g][h][1][:], start=(g == 0), stop=(g == 1),
            )

        y = {}
        for h in range(2):
            for u in range(N // P):
                y[h, u] = psum.tile([P, HALF], F32, name="bank")
                y_pass(y[h, u], u, h, 0)
        for h in range(2):
            cols = slice(h * HALF, (h + 1) * HALF)
            for pair in range(2):
                result = ring.tile([P, 2, HALF], F32, name="result", bufs=4)
                for side in range(2):
                    u = 2 * pair + side
                    y_pass(y[h, u], u, h, 1)
                    nc.vector.tensor_tensor(result[:, side, :], y[h, u][:], gate[:, u, cols], ALU.mult)
                stored = out[2 * pair * P : 2 * (pair + 1) * P, cols]
                nc.sync.dma_start(stored.rearrange("(side p) j -> p side j", p=P), result[:])
